import numpy as np, ml_dtypes
CORES = [17,57,65,89,97,121]
N = 6
KB, QP, ROOT = 1, 64, 2
def setup_inputs(rng):
    return {"q": rng.standard_normal((N, 128, QP), dtype=np.float32).astype(ml_dtypes.bfloat16), "k": rng.standard_normal((N, 128, KB * 128), dtype=np.float32).astype(ml_dtypes.bfloat16), "v": rng.standard_normal((N, 128, KB * 128), dtype=np.float32).astype(ml_dtypes.bfloat16)}
def setup_inputs_big(rng):
    d = setup_inputs(rng)
    for k in ("q", "k", "v"): d[k] = (d[k].astype(np.float32) * 1024.0).astype(d[k].dtype)
    return d
def setup_inputs_small(rng):
    d = setup_inputs(rng)
    for k in ("q", "k", "v"): d[k] = (d[k].astype(np.float32) * (1 / 1024.0)).astype(d[k].dtype)
    return d
def setup_inputs_apart(rng):
    d = setup_inputs(rng)
    f = (10.0 ** rng.permutation(np.linspace(-1.5, 1.5, N))).astype(np.float32).reshape(N, 1, 1)
    for k in ("q", "k", "v"): d[k] = (d[k].astype(np.float32) * f).astype(d[k].dtype)
    return d
def reference(q, k, v):
    Q, K, V = q.astype(np.float64), k.astype(np.float64), v.astype(np.float64)
    o = np.zeros((128, QP))
    for j in range(N):
        for b in range(KB):
            o += V[j][:, 128 * b:128 * b + 128].T @ np.maximum(K[j][:, 128 * b:128 * b + 128].T @ Q[ROOT], 0.0)
    y = np.full((N, 128, QP), np.nan)
    y[ROOT] = o
    return {"y": y.astype(ml_dtypes.bfloat16 if q.dtype != np.float64 else np.float64)}

from concourse.bass import DstId, RemoteDMATransfer
from concourse.mybir import AluOpType

N = 6
P = 128
QP = 64

HAND_ENGINES = 4
PASS_ENGINES = 8
DIRECT_ENGINES = 4

SCRATCH = {
    "stage": ("dram", [2, P, P], "bfloat16"),
    "q_sb": ("sbuf", [P, QP], "bfloat16"),
    "k_sb": ("sbuf", [P, N * P], "bfloat16"),
    "v_sb": ("sbuf", [P, N * P], "bfloat16"),
    "s_sb": ("sbuf", [P, N * QP], "bfloat16"),
    "zero": ("sbuf", [P, QP], "float32"),
    "y_sb": ("sbuf", [P, QP], "bfloat16"),
    "o_ps": ("psum", [P, 512], "float32"),
}
for _j in range(N):
    SCRATCH["s_ps%d" % _j] = ("psum", [P, 512], "float32")

SEMAPHORES = ["ld", "got", "sent", "zf", "od", "yc", "st"]
for _j in range(N):
    SEMAPHORES += ["ak%d" % _j, "av%d" % _j, "mm%d" % _j, "rl%d" % _j]


def _bits(mask):
    return [b for b in range(mask.bit_length()) if (mask >> b) & 1]


def _mask_of(bits):
    m = 0
    for b in bits:
        m |= 1 << b
    return m


def _plan(T, topo):
    root = T.cores[T.root]
    every = range(topo.CHIPS * topo.CORES_PER_CHIP)
    plan = {}
    for j, c in enumerate(T.cores):
        if c == root:
            continue
        if topo.may_write(c, root):
            plan[j] = None
            continue
        can = [x for x in every
               if topo.chip(x) == topo.chip(c) and T.rank_of(x) is None and topo.may_write(x, root)]
        near = [x for x in can if topo.die(x) == topo.die(c)]
        far = [x for x in can if topo.die(x) != topo.die(c)]
        plan[j] = (near[0], far[0])
    return plan


def _transfer(topo, dst_core, mask, sem, src, dst):
    rid, pid, _ = topo.addr(dst_core)
    return RemoteDMATransfer(dst_ids=[DstId(rid=rid, pnc=pid)], dma_engine_mask=mask, remote_sem=sem, src=src, dst=dst)


def _root_slot(T, j):
    return T.k_sb[:, j * P:(j + 1) * P], T.v_sb[:, j * P:(j + 1) * P]


def rank_program(g, core, T, topo):
    root = T.cores[T.root]
    plan = _plan(T, topo)
    rank = T.rank_of(core)

    if rank is None:
        for j, helpers in plan.items():
            if helpers is None or core not in helpers:
                continue
            piece = helpers.index(core)
            g.wait_ge(T.sem.got, HAND_ENGINES)
            rid, pid, _ = topo.addr(root)
            g.remote_dma(out_ap=_root_slot(T, j)[piece], in_ap=T.stage[piece],
                         remote_sem=T.sem[("ak%d", "av%d")[piece] % j], local_sem=T.sem.sent,
                         pid=pid, routing_id=rid,
                         dma_engine_mask=_mask_of(_bits(topo.mask(core, root))[:PASS_ENGINES]))
            g.wait_ge(T.sem.sent, PASS_ENGINES)
        return

    if core != root:
        g.sync.dma_start(out=T.stage[0], in_=T.k[:]).then_inc(T.sem.ld, 16)
        g.scalar.dma_start(out=T.stage[1], in_=T.v[:]).then_inc(T.sem.ld, 16)
        g.wait_ge(T.sem.ld, 32)
        helpers = plan[rank]
        if helpers is None:
            n = DIRECT_ENGINES
            bits = _bits(topo.mask(core, root))
            ks, vs = _root_slot(T, rank)
            g.remote_dma_fused([
                _transfer(topo, root, _mask_of(bits[0:n]), T.sem["ak%d" % rank], T.stage[0], ks),
                _transfer(topo, root, _mask_of(bits[n:2 * n]), T.sem["av%d" % rank], T.stage[1], vs),
            ], local_sem=T.sem.sent)
        else:
            n = HAND_ENGINES
            bits = _bits(topo.mask(core, helpers[0]) & topo.mask(core, helpers[1]))
            g.remote_dma_fused([
                _transfer(topo, helpers[0], _mask_of(bits[0:2 * n:2]), T.sem.got, T.stage[0], T.stage[0]),
                _transfer(topo, helpers[1], _mask_of(bits[1:2 * n:2]), T.sem.got, T.stage[1], T.stage[1]),
            ], local_sem=T.sem.sent)
        g.wait_ge(T.sem.sent, 2 * n)
        return

    te, ve = g.tensor, g.vector
    ve.memset(T.zero[:], 0.0).then_inc(T.sem.zf, 1)
    ks, vs = _root_slot(T, rank)
    g.sync.dma_start(out=T.q_sb[:], in_=T.q[:]).then_inc(T.sem.ld, 16)
    g.scalar.dma_start(out=ks, in_=T.k[:]).then_inc(T.sem.ld, 16)
    g.sync.dma_start(out=vs, in_=T.v[:]).then_inc(T.sem.ld, 16)
    te.wait_ge(T.sem.ld, 48)
    ve.wait_ge(T.sem.zf, 1)

    waves = [[rank],
             [j for j in plan if plan[j] is None],
             [j for j in plan if plan[j] is not None]]
    waves = [w for w in waves if w]
    order = [j for w in waves for j in w]
    for w in waves:
        for j in w:
            kj, _ = _root_slot(T, j)
            if j != rank:
                te.wait_ge(T.sem["ak%d" % j], DIRECT_ENGINES if plan[j] is None else PASS_ENGINES)
            s_ps = T["s_ps%d" % j]
            te.matmul(out=s_ps[:, 0:QP], lhsT=kj, rhs=T.q_sb[:], start=True, stop=True).then_inc(T.sem["mm%d" % j], 1)
            ve.wait_ge(T.sem["mm%d" % j], 1)
            ve.tensor_tensor(out=T.s_sb[:, j * QP:(j + 1) * QP], in0=s_ps[:, 0:QP], in1=T.zero[:],
                             op=AluOpType.max).then_inc(T.sem["rl%d" % j], 1)
        for j in w:
            _, vj = _root_slot(T, j)
            if j != rank:
                te.wait_ge(T.sem["av%d" % j], DIRECT_ENGINES if plan[j] is None else PASS_ENGINES)
            te.wait_ge(T.sem["rl%d" % j], 1)
            mm = te.matmul(out=T.o_ps[:, 0:QP], lhsT=vj, rhs=T.s_sb[:, j * QP:(j + 1) * QP],
                           start=(j == order[0]), stop=(j == order[-1]))
            if j == order[-1]:
                mm.then_inc(T.sem.od, 1)
    ve.wait_ge(T.sem.od, 1)
    ve.tensor_copy(out=T.y_sb[:], in_=T.o_ps[:, 0:QP]).then_inc(T.sem.yc, 1)
    g.sync.wait_ge(T.sem.yc, 1)
    g.sync.dma_start(out=T.y[:], in_=T.y_sb[:]).then_inc(T.sem.st, 16)
    g.sync.wait_ge(T.sem.st, 16)
